import numpy as np
import ml_dtypes


def mxq(x, axis, fmt="e4m3"):
    dtype, down = {"e4m3": (ml_dtypes.float8_e4m3fn, 7), "e5m2": (ml_dtypes.float8_e5m2, 14)}[fmt]
    v = np.moveaxis(np.asarray(x, np.float32).astype(ml_dtypes.bfloat16).astype(np.float64), axis, -1)
    blocks = v.reshape(v.shape[:-1] + (-1, 32))
    amax = np.abs(blocks).max(-1, keepdims=True)
    byte = np.maximum(np.where(amax > 0, np.frexp(amax)[1] - 1 + 127, 0) - down, 1)
    scale = np.exp2(byte - 127.0)
    codes = (blocks / scale).astype(np.float32).astype(dtype).astype(np.float64)
    return np.moveaxis((codes * scale).reshape(v.shape), -1, axis)


WIDE = False


def mx_kscale(k):
    if not WIDE:
        return np.ones(k)
    levels = np.array([10, -10, 5, -5, 0])
    if k % 512:
        return np.exp2(np.random.permutation(np.resize(levels, k // 32))).repeat(32)
    a = np.empty((k // 512, 16))
    for p in range(k // 512):
        a[p, :8] = np.random.permutation(np.resize(levels, 8))
        for g in range(8):
            far = levels[np.abs(levels - a[p, g]) >= 10]
            a[p, g + 8] = far[np.random.randint(len(far))]
    return np.exp2(a.ravel()).repeat(32)


def f64(x):
    return np.asarray(x).astype(np.float64)


def striped(idx):
    return np.tile(idx.reshape(-1, 16).T, (8, 1)).astype(np.uint16)


def unstriped(offs):
    return offs[:16].T.reshape(-1).astype(np.int64)


def striped8(idx):
    return np.concatenate([x.reshape(-1, 16).T for x in idx]).astype(np.uint16)


def runs(offs, k):
    lists = np.stack([offs[16 * r : 16 * r + 16].T.reshape(-1) for r in range(8)]).astype(np.int64)
    return lists[np.arange(k) % 512 // 64]


def pack_weight(w):
    k, n = w.shape
    w = f64(np.asarray(w, np.float32).astype(ml_dtypes.bfloat16)).reshape(k // 32, 32, n)
    amax = np.abs(w).max(1)
    byte = np.clip(np.where(amax > 0, np.frexp(amax)[1] - 1 + 127 - 7, 1), 1, 254)
    scaled = (w * np.exp2(127.0 - byte)[:, None, :]).reshape(k, n).astype(np.float32)
    words = np.ascontiguousarray(scaled.reshape(k // 512, 128, 4, n).transpose(0, 1, 3, 2)).astype(ml_dtypes.float8_e4m3fn).view(np.uint8)
    return words, np.ascontiguousarray(byte.astype(np.uint8).reshape(k // 512, 16, n))


def unpack_weight(words, scales):
    g, p, n, _ = words.shape
    vals = np.ascontiguousarray(words).view(ml_dtypes.float8_e4m3fn).astype(np.float64) * np.repeat(np.exp2(scales.astype(np.float64) - 127.0), 8, axis=1)[..., None]
    return vals.transpose(0, 1, 3, 2).reshape(g * 512, n)


def sigmoid(v):
    return 1.0 / (1.0 + np.exp(-np.maximum(v, -700.0)))

def planes(y):
    n, m = y.shape
    v = y.astype(np.float32).astype(ml_dtypes.bfloat16).astype(np.float64).reshape(n // 32, 32, m)
    top = np.abs(v).max(1)
    byte = np.clip(np.where(top > 0, np.frexp(top)[1] - 1 + 127 - 7, 1), 1, 254)
    codes = (v * np.exp2(127.0 - byte)[:, None, :]).reshape(n, m).astype(np.float32).astype(ml_dtypes.float8_e4m3fn).view(np.uint8)
    words = codes.reshape(n // 512, 128, 4, m).transpose(0, 1, 3, 2)
    return np.ascontiguousarray(words), np.ascontiguousarray(byte.astype(np.uint8).reshape(n // 512, 16, m))


K, T, S, N, G, H, W = 512, 1024, 512, 512, 2048, 512, 256


def setup_inputs():
    n = np.random.standard_normal
    s = mx_kscale(K)[:, None]
    u = mx_kscale(S)
    packed_xT = pack_weight(n((K, T)) * s)
    packed_dT = pack_weight(n((K, G)) / s)
    packed_w1 = pack_weight(n((H, N)) / np.sqrt(2 * H) / u[:, None])
    packed_w2 = pack_weight(n((K, N)) / np.sqrt(2 * K) / s)
    perm = np.random.permutation(S)
    return {
        "x_words": packed_xT[0],
        "x_scales": packed_xT[1],
        "d_words": packed_dT[0],
        "d_scales": packed_dT[1],
        "sl": np.random.uniform(1.0, 2.0, (H, 1)).astype(np.float32),
        "th": (0.5 * n((H, 1))).astype(np.float32),
        "gn": (np.random.uniform(0.5, 1.5, (H, 1)) * u[:, None]).astype(np.float32),
        "w1_words": packed_w1[0],
        "w1_scales": packed_w1[1],
        "w2_words": packed_w2[0],
        "w2_scales": packed_w2[1],
        "sl2": np.random.uniform(1.0, 2.0, (N, 1)).astype(np.float32),
        "th2": (0.5 * n((N, 1))).astype(np.float32),
        "offs": striped(np.random.permutation(T)[:S]),
        "k1": striped8(np.random.randint(0, G, (8, H))),
        "n1": striped(perm[:W]),
        "n2": striped(perm[W:]),
        "two": striped(np.random.permutation(T)[:S]),
        "n3": striped(np.random.permutation(S)),
        "n4": striped(np.random.permutation(S)),
    }


def reference(x_words, x_scales, d_words, d_scales, sl, th, gn, w1_words, w1_scales, w2_words, w2_scales, sl2, th2, offs, k1, n1, n2, two, n3, n4):
    d_k1 = unpack_weight(d_words, d_scales)[np.arange(K)[:, None], runs(k1, K)]
    xq = unpack_weight(x_words, x_scales)[:, unstriped(offs)]
    h = 0.0625 * (d_k1.T @ xq)
    pb = h[:, unstriped(n2)]
    sg = sigmoid(f64(sl) * (h[:, unstriped(n1)] - f64(th)))
    rb = pb - sg
    pa = h[:, unstriped(n1)]
    sg2 = sigmoid(f64(sl) * (h[:, unstriped(n2)] - f64(th)))
    ra = pa * sg2
    ds = np.zeros((H, S))
    ds[:, unstriped(n1)] = ra
    dt = ds.copy()
    dt[:, unstriped(n2)] = rb
    z = f64(gn) * dt
    x_two = unpack_weight(x_words, x_scales)[:, unstriped(two)]
    h2 = unpack_weight(w1_words, w1_scales).T @ mxq(z, 0, "e4m3") + unpack_weight(w2_words, w2_scales).T @ x_two
    pa2 = h2[:, unstriped(n3)]
    sg3 = sigmoid(f64(sl2) * (h2[:, unstriped(n4)] - f64(th2)))
    out_0 = pa2 + sg3 * (h2 - pa2)
    return (out_0,) + planes(out_0)

@@ -1,0 +1,280 @@
+from contextlib import ExitStack
+
+import concourse.mybir as mybir
+
+K, T, S, N, G, H, W = 512, 1024, 512, 512, 2048, 512, 256
+FLOPS = 3 * 2 * 512 * 512 * 512
+
+F32 = mybir.dt.float32
+BF16 = mybir.dt.bfloat16
+I32 = mybir.dt.int32
+U32 = mybir.dt.uint32
+U16 = mybir.dt.uint16
+U8 = mybir.dt.uint8
+FP8X4 = mybir.dt.float8_e4m3fn_x4
+ALU = mybir.AluOpType
+ACT = mybir.ActivationFunctionType
+
+P = 128
+PACK = 4
+HALF = S // 2
+CHUNKS = ((0, 256), (256, 128), (384, 128))
+
+
+def tile_picked_pqmixeodebl_none_po_kernel(
+    tc, x_words, x_scales, d_words, d_scales, sl, th, gn, w1_words, w1_scales, w2_words, w2_scales,
+    sl2, th2, offs, k1, n1, n2, two, n3, n4, out_0, out_1, out_2,
+):
+    nc = tc.nc
+
+    def entries(lst, start, count):
+        return lst[:, start // 16 : (start + count) // 16]
+
+    def words_view(dram):
+        return dram[0].rearrange("p n t -> p (n t)").bitcast(I32)
+
+    def dealt_src(tile):
+        return tile.rearrange("p (m t) -> p t m", t=PACK)
+
+    def dealt_dst(tile):
+        return tile.rearrange("p (t m) -> p t m", t=PACK)
+
+    with ExitStack() as ctx:
+        keep = ctx.enter_context(tc.tile_pool(name="keep", bufs=1))
+        psum = ctx.enter_context(tc.psum_pool(name="psum", bufs=8))
+
+        def load_list(name, dram):
+            tile = keep.tile(list(dram.shape), U16, name=name)
+            nc.sync.dma_start(tile[:], dram)
+            return tile
+
+        def load_rows(queue, name, dram):
+            tile = keep.tile([P, PACK], F32, name=name)
+            queue.dma_start(tile[:], dram.rearrange("(p t) o -> p (t o)", t=PACK))
+            return tile
+
+        k1_t = load_list("k1_t", k1)
+        d_sc_win = keep.tile([P, G], U8, name="d_sc_win")
+        nc.scalar.dma_start(
+            d_sc_win[:].bitcast(I32), d_scales[0].bitcast(I32).unsqueeze(1).broadcast_to([16, 8, G // 4])
+        )
+        offs_t = load_list("offs_t", offs)
+        d_win = keep.tile([P, G], U32, name="d_win", tag="big")
+        nc.scalar.dma_start(d_win[:].bitcast(I32), words_view(d_words))
+        x_sc_win = keep.tile([P, T], U8, name="x_sc_win", tag="x_sc_win")
+        for q in range(4):
+            nc.sync.dma_start(
+                x_sc_win[:].bitcast(I32)[32 * q : 32 * q + 32, :],
+                x_scales[0].bitcast(I32)[4 * q : 4 * q + 4, :].unsqueeze(0).broadcast_to([8, 4, T // 4]),
+            )
+        x_win = keep.tile([P, T], U32, name="x_win", tag="x_win")
+        nc.scalar.dma_start(x_win[:].bitcast(I32), words_view(x_words))
+        n2_t = load_list("n2_t", n2)
+        n1_t = load_list("n1_t", n1)
+        d_sc_placed = keep.tile([P, H], U8, name="d_sc_placed")
+        nc.vector.memset(d_sc_placed[:].bitcast(I32), 0)
+        w_sc_raw = keep.tile([P, N], U8, name="w_sc_raw", tag="w_sc_raw")
+        nc.vector.memset(w_sc_raw[:].bitcast(I32), 0)
+
+        def gate_bias(name, slope, threshold):
+            prod = keep.tile([P, PACK], F32, name=name + "_prod", tag=name + "_prod")
+            bias = keep.tile([P, PACK], F32, name=name)
+            nc.gpsimd.tensor_tensor(prod[:], slope[:], threshold[:], ALU.mult)
+            nc.gpsimd.tensor_scalar(bias[:], prod[:], -1.0, 0.0, ALU.mult, ALU.add)
+            return bias
+
+        sl_t = load_rows(nc.gpsimd, "sl_t", sl)
+        th_t = load_rows(nc.gpsimd, "th_t", th)
+        gn_t = load_rows(nc.gpsimd, "gn_t", gn)
+        bias1 = gate_bias("bias1", sl_t, th_t)
+        for i, dram in enumerate((w1_scales, w2_scales)):
+            for q in range(4):
+                nc.gpsimd.dma_start(
+                    w_sc_raw[:].bitcast(I32)[32 * q + 4 * i : 32 * q + 4 * i + 4, :],
+                    dram[0].bitcast(I32)[4 * q : 4 * q + 4, :],
+                )
+
+        d_sc_got = keep.tile([P, H], U8, name="d_sc_got")
+        nc.vector.tensor_copy(d_sc_got[:], d_sc_win[:].indirect(k1_t[:]))
+        for j in range(4):
+            nc.scalar.dma_start(d_sc_placed[:].bitcast(I32)[j:P:32, :], d_sc_got[:].bitcast(I32)[8 * j : P : 32, :])
+
+        x_sc = keep.tile([P, S], U8, name="x_sc", tag="x_sc", align_bytes=64)
+        nc.vector.tensor_copy(x_sc[:], x_sc_win[:].indirect(offs_t[:]))
+        d_got = keep.tile([P, H], U32, name="d_got")
+        nc.vector.tensor_copy(d_got[:], d_win[:].indirect(k1_t[:]))
+        d_w = keep.tile([P, H], U32, name="d_w", align_bytes=64)
+        d_sc = keep.tile([P, H], U8, name="d_sc", align_bytes=64)
+        x_w = [keep.tile([P, HALF], U32, name=f"x_w{c}", tag=f"x_w{c}", align_bytes=64) for c in range(2)]
+        nc.vector.tensor_copy(dealt_dst(d_w[:])[:, 0, :], dealt_src(d_got[:])[:, 0, :])
+        nc.vector.tensor_copy(x_w[0][:], x_win[:].indirect(entries(offs_t, 0, HALF)))
+        nc.vector.tensor_copy(dealt_dst(d_sc[:])[:, 0, :], dealt_src(d_sc_placed[:])[:, 0, :])
+        nc.vector.tensor_copy(x_w[1][:], x_win[:].indirect(entries(offs_t, HALF, HALF)))
+
+        def first_product(t, c, acc):
+            nc.tensor.matmul_mx(
+                out=acc,
+                lhsT=d_w[:, t * P : (t + 1) * P].bitcast(FP8X4),
+                lhsT_scale=d_sc[:, t * P : (t + 1) * P],
+                rhs=x_w[c][:].bitcast(FP8X4),
+                rhs_scale=x_sc[:, c * HALF : (c + 1) * HALF],
+                start=True,
+                stop=True,
+            )
+
+        h = [keep.tile([P, S], F32, name=f"h{t}") for t in range(PACK)]
+        for c in range(2):
+            acc = psum.tile([P, HALF], F32, name="acc", tag="acc")
+            first_product(0, c, acc[:])
+            nc.vector.tensor_scalar(h[0][:, c * HALF : (c + 1) * HALF], acc[:], 0.0625, None, ALU.mult)
+        nc.vector.tensor_copy(dealt_dst(d_w[:])[:, 1:, :], dealt_src(d_got[:])[:, 1:, :])
+        nc.vector.tensor_copy(dealt_dst(d_sc[:])[:, 1:, :], dealt_src(d_sc_placed[:])[:, 1:, :])
+        for t in range(1, PACK):
+            acc = psum.tile([P, S], F32, name="acc", tag="acc")
+            for c in range(2):
+                first_product(t, c, acc[:, c * HALF : (c + 1) * HALF])
+            nc.vector.tensor_scalar(h[t][:], acc[:], 0.0625, None, ALU.mult)
+
+        two_t = load_list("two_t", two)
+        n3_t = load_list("n3_t", n3)
+        n4_t = load_list("n4_t", n4)
+        sl2_t = load_rows(nc.gpsimd, "sl2_t", sl2)
+        th2_t = load_rows(nc.gpsimd, "th2_t", th2)
+        bias2 = gate_bias("bias2", sl2_t, th2_t)
+
+        w_raw = keep.tile([P, 2, N], U32, name="w_raw", tag="big")
+        for i, dram in enumerate((w2_words, w1_words)):
+            nc.sync.dma_start(w_raw[:, i, :].bitcast(I32), words_view(dram))
+
+        z = [keep.tile([P, HALF, PACK], BF16, name=f"z{c}", align_bytes=64) for c in range(2)]
+
+        def stage_one(t, picked_tag, ra_tag, rb_tag):
+            scale, bias = sl_t[:, t : t + 1], bias1[:, t : t + 1]
+            sg2 = keep.tile([P, W], F32, name=f"sg2_{t}")
+            picked = keep.tile([P, 2, W], F32, name=f"picked{t}", tag=picked_tag)
+            pa, pb = picked[:, 0, :], picked[:, 1, :]
+            sg = keep.tile([P, W], F32, name=f"sg{t}")
+            ra = keep.tile([P, W], F32, name=f"ra{t}", tag=ra_tag)
+            rb = keep.tile([P, W], F32, name=f"rb{t}", tag=rb_tag)
+            dt = keep.tile([P, S], F32, name=f"dt{t}")
+            nc.scalar.activation(sg2[:], h[t][:].indirect(n2_t[:]), ACT.Sigmoid, bias=bias, scale=scale)
+            nc.scalar.activation(pa, h[t][:].indirect(n1_t[:]), ACT.Copy)
+            nc.vector.tensor_tensor(ra[:], pa, sg2[:], ALU.mult)
+            nc.scalar.activation(sg[:], h[t][:].indirect(n1_t[:]), ACT.Sigmoid, bias=bias, scale=scale)
+            nc.scalar.activation(pb, h[t][:].indirect(n2_t[:]), ACT.Copy)
+            nc.vector.tensor_tensor(rb[:], pb, sg[:], ALU.subtract)
+            nc.scalar.activation(dt[:].indirect(n1_t[:]), ra[:], ACT.Copy)
+            nc.scalar.activation(dt[:].indirect(n2_t[:]), rb[:], ACT.Copy)
+            return dt
+
+        def round_z(t, dt, c):
+            nc.vector.tensor_scalar(
+                z[c][:, :, t], dt[:, c * HALF : (c + 1) * HALF], gn_t[:, t : t + 1], None, ALU.mult
+            )
+
+        dt = stage_one(0, "bias1_prod", "ra0", "rb0")
+        for c in range(2):
+            round_z(0, dt, c)
+
+        x2_w = [keep.tile([P, HALF], U32, name=f"x2_w{c}", tag=f"x_w{c}", align_bytes=64) for c in range(2)]
+        x2_sc = keep.tile([P, S], U8, name="x2_sc", tag="x_sc", align_bytes=64)
+        for c in range(2):
+            nc.vector.tensor_copy(x2_w[c][:], x_win[:].indirect(entries(two_t, c * HALF, HALF)))
+            nc.vector.tensor_copy(x2_sc[:, c * HALF : (c + 1) * HALF], x_sc_win[:].indirect(entries(two_t, c * HALF, HALF)))
+
+        dt = stage_one(1, "picked1", "ra1", "rb1")
+        for c in range(2):
+            round_z(1, dt, c)
+
+        w2_w = keep.tile([P, N], U32, name="w2_w", align_bytes=64)
+        w1_w = keep.tile([P, N], U32, name="w1_w", align_bytes=64)
+        w_sc = keep.tile([P, N], U8, name="w_sc", align_bytes=64)
+        nc.vector.tensor_copy(dealt_dst(w2_w[:]), dealt_src(w_raw[:, 0, :]))
+        nc.vector.tensor_copy(dealt_dst(w_sc[:]), dealt_src(w_sc_raw[:]))
+        nc.vector.tensor_copy(dealt_dst(w1_w[:]), dealt_src(w_raw[:, 1, :]))
+
+        acc2 = {}
+        for c in range(2):
+            for t in range(PACK):
+                acc2[c, t] = psum.tile([P, HALF], F32, name="acc", tag="acc")
+                nc.tensor.matmul_mx(
+                    out=acc2[c, t][:],
+                    lhsT=w2_w[:, t * P : (t + 1) * P].bitcast(FP8X4),
+                    lhsT_scale=w_sc[4:P, t * P : (t + 1) * P],
+                    rhs=x2_w[c][:].bitcast(FP8X4),
+                    rhs_scale=x2_sc[:, c * HALF : (c + 1) * HALF],
+                    start=True,
+                    stop=False,
+                )
+
+        dt = stage_one(2, "picked2", "x_sc_win", "x_win")
+        for c in range(2):
+            round_z(2, dt, c)
+        dt = stage_one(3, "picked3", "w_sc_raw", "big")
+
+        h2 = [keep.tile([P, S], F32, name=f"h2_{t}") for t in range(PACK)]
+        z_w = [keep.tile([P, HALF], U32, name=f"z_w{c}", align_bytes=64) for c in range(2)]
+        z_sc = [keep.tile([P, HALF], U8, name=f"z_sc{c}", align_bytes=64) for c in range(2)]
+        for c in range(2):
+            round_z(3, dt, c)
+            nc.vector.quantize_mx(
+                out=z_w[c][:].bitcast(FP8X4), scales=z_sc[c][:], in_=z[c][:].rearrange("p w j -> p (w j)")
+            )
+        for t in range(PACK):
+            for c in range(2):
+                nc.tensor.matmul_mx(
+                    out=acc2[c, t][:],
+                    lhsT=w1_w[:, t * P : (t + 1) * P].bitcast(FP8X4),
+                    lhsT_scale=w_sc[:, t * P : (t + 1) * P],
+                    rhs=z_w[c][:].bitcast(FP8X4),
+                    rhs_scale=z_sc[c][:],
+                    start=False,
+                    stop=True,
+                )
+        for t in range(PACK):
+            for c in range(2):
+                dst = h2[t][:, c * HALF : (c + 1) * HALF]
+                if c == 0 or t == 0:
+                    nc.scalar.copy(dst, acc2[c, t][:])
+                else:
+                    nc.vector.tensor_copy(dst, acc2[c, t][:])
+
+        out_rows = out_0.rearrange("(p t) j -> p t j", t=PACK)
+        o_w = keep.tile([P, S], U32, name="o_w", align_bytes=64)
+        o_sc = keep.tile([P, S], U8, name="o_sc", align_bytes=64)
+        for ci, (j0, cw) in enumerate(CHUNKS):
+            cols = slice(j0, j0 + cw)
+            res = keep.tile([P, PACK, cw], F32, name=f"res{ci}")
+            pa2 = keep.tile([P, PACK, cw], F32, name=f"pa2_{ci}")
+            sg3 = keep.tile([P, PACK, cw], F32, name=f"sg3_{ci}")
+            diff = keep.tile([P, PACK, cw], F32, name=f"diff_{ci}")
+            prod = keep.tile([P, PACK, cw], F32, name=f"prod_{ci}")
+            group = 2
+            for t in range(PACK):
+                picked = h2[t][:].indirect(entries(n3_t, j0, cw))
+                if ci == 0 and t < 2:
+                    nc.vector.tensor_copy(pa2[:, t, :], picked)
+                else:
+                    nc.scalar.activation(pa2[:, t, :], picked, ACT.Copy)
+                nc.scalar.activation(
+                    sg3[:, t, :], h2[t][:].indirect(entries(n4_t, j0, cw)), ACT.Sigmoid,
+                    bias=bias2[:, t : t + 1], scale=sl2_t[:, t : t + 1],
+                )
+                nc.vector.tensor_tensor(diff[:, t, :], h2[t][:, cols], pa2[:, t, :], ALU.subtract)
+                if (t + 1) % group == 0:
+                    rows = slice(t + 1 - group, t + 1)
+                    nc.vector.tensor_tensor(prod[:, rows, :], sg3[:, rows, :], diff[:, rows, :], ALU.mult)
+                    nc.vector.tensor_tensor(res[:, rows, :], pa2[:, rows, :], prod[:, rows, :], ALU.add)
+            nc.sync.dma_start(out_rows[:, :, cols], res[:])
+            rounded = keep.tile([P, cw, PACK], BF16, name=f"rounded{ci}", align_bytes=64)
+            dst = rounded[:].rearrange("p (c i) t -> p c t i", i=4)
+            src = res[:].rearrange("p t (c i) -> p c t i", i=4)
+            nc.vector.tensor_copy(dst, src)
+            nc.vector.quantize_mx(
+                out=o_w[:, cols].bitcast(FP8X4), scales=o_sc[:, cols], in_=rounded[:].rearrange("p w j -> p (w j)")
+            )
+            nc.sync.dma_start(words_view(out_1)[:, cols], o_w[:, cols].bitcast(I32))
+        for q in range(4):
+            nc.scalar.dma_start(
+                out_2[0].bitcast(I32)[4 * q : 4 * q + 4, :], o_sc[:].bitcast(I32)[32 * q : 32 * q + 4, :]
+            )

@@ -48,8 +48,8 @@ def tile_picked_pqmixeodebl_none_po_kernel(
             nc.sync.dma_start(tile[:], dram)
             return tile
 
-        def load_rows(queue, name, dram):
-            tile = keep.tile([P, PACK], F32, name=name)
+        def load_rows(queue, name, dram, tag):
+            tile = keep.tile([P, PACK], F32, name=name, tag=tag, align_bytes=64)
             queue.dma_start(tile[:], dram.rearrange("(p t) o -> p (t o)", t=PACK))
             return tile
 
@@ -59,57 +59,44 @@ def tile_picked_pqmixeodebl_none_po_kernel(
             d_sc_win[:].bitcast(I32), d_scales[0].bitcast(I32).unsqueeze(1).broadcast_to([16, 8, G // 4])
         )
         offs_t = load_list("offs_t", offs)
-        d_win = keep.tile([P, G], U32, name="d_win", tag="big")
-        nc.scalar.dma_start(d_win[:].bitcast(I32), words_view(d_words))
-        x_sc_win = keep.tile([P, T], U8, name="x_sc_win", tag="x_sc_win")
+        x_sc_win = keep.tile([P, T], U8, name="x_sc_win")
         for q in range(4):
             nc.sync.dma_start(
                 x_sc_win[:].bitcast(I32)[32 * q : 32 * q + 32, :],
                 x_scales[0].bitcast(I32)[4 * q : 4 * q + 4, :].unsqueeze(0).broadcast_to([8, 4, T // 4]),
             )
-        x_win = keep.tile([P, T], U32, name="x_win", tag="x_win")
+        x_win = keep.tile([P, T], U32, name="x_win", tag="x_win", align_bytes=64)
         nc.scalar.dma_start(x_win[:].bitcast(I32), words_view(x_words))
+        d_win = keep.tile([P, G], U32, name="d_win", tag="big", align_bytes=64)
+        nc.scalar.dma_start(d_win[:].bitcast(I32), words_view(d_words))
         n2_t = load_list("n2_t", n2)
         n1_t = load_list("n1_t", n1)
-        d_sc_placed = keep.tile([P, H], U8, name="d_sc_placed")
-        nc.vector.memset(d_sc_placed[:].bitcast(I32), 0)
-        w_sc_raw = keep.tile([P, N], U8, name="w_sc_raw", tag="w_sc_raw")
-        nc.vector.memset(w_sc_raw[:].bitcast(I32), 0)
+        d_sc = keep.tile([P, H], U8, name="d_sc", tag="d_sc", align_bytes=64)
+        nc.vector.memset(d_sc[:].bitcast(I32), 0)
+        sl_t = load_rows(nc.gpsimd, "sl_t", sl, "sl_t")
+        th_t = load_rows(nc.gpsimd, "th_t", th, "th_t")
 
-        def gate_bias(name, slope, threshold):
-            prod = keep.tile([P, PACK], F32, name=name + "_prod", tag=name + "_prod")
-            bias = keep.tile([P, PACK], F32, name=name)
-            nc.gpsimd.tensor_tensor(prod[:], slope[:], threshold[:], ALU.mult)
-            nc.gpsimd.tensor_scalar(bias[:], prod[:], -1.0, 0.0, ALU.mult, ALU.add)
+        def gate_bias(name, slope, threshold, tag):
+            bias = keep.tile([P, PACK], F32, name=name, tag=tag, align_bytes=64)
+            nc.vector.scalar_tensor_tensor(bias[:], slope[:], -1.0, threshold[:], ALU.mult, ALU.mult)
             return bias
-
-        sl_t = load_rows(nc.gpsimd, "sl_t", sl)
-        th_t = load_rows(nc.gpsimd, "th_t", th)
-        gn_t = load_rows(nc.gpsimd, "gn_t", gn)
-        bias1 = gate_bias("bias1", sl_t, th_t)
-        for i, dram in enumerate((w1_scales, w2_scales)):
-            for q in range(4):
-                nc.gpsimd.dma_start(
-                    w_sc_raw[:].bitcast(I32)[32 * q + 4 * i : 32 * q + 4 * i + 4, :],
-                    dram[0].bitcast(I32)[4 * q : 4 * q + 4, :],
-                )
 
         d_sc_got = keep.tile([P, H], U8, name="d_sc_got")
         nc.vector.tensor_copy(d_sc_got[:], d_sc_win[:].indirect(k1_t[:]))
+        d_sc_dealt = keep.tile([P, H], U8, name="d_sc_dealt", tag="w_sc_raw", align_bytes=64)
+        nc.vector.tensor_copy(dealt_dst(d_sc_dealt[:]), dealt_src(d_sc_got[:]))
         for j in range(4):
-            nc.scalar.dma_start(d_sc_placed[:].bitcast(I32)[j:P:32, :], d_sc_got[:].bitcast(I32)[8 * j : P : 32, :])
+            nc.scalar.dma_start(d_sc[:].bitcast(I32)[j:P:32, :], d_sc_dealt[:].bitcast(I32)[8 * j : P : 32, :])
 
-        x_sc = keep.tile([P, S], U8, name="x_sc", tag="x_sc", align_bytes=64)
+        x_sc = keep.tile([P, S], U8, name="x_sc", align_bytes=64)
         nc.vector.tensor_copy(x_sc[:], x_sc_win[:].indirect(offs_t[:]))
-        d_got = keep.tile([P, H], U32, name="d_got")
-        nc.vector.tensor_copy(d_got[:], d_win[:].indirect(k1_t[:]))
-        d_w = keep.tile([P, H], U32, name="d_w", align_bytes=64)
-        d_sc = keep.tile([P, H], U8, name="d_sc", align_bytes=64)
         x_w = [keep.tile([P, HALF], U32, name=f"x_w{c}", tag=f"x_w{c}", align_bytes=64) for c in range(2)]
+        for c in range(2):
+            nc.vector.tensor_copy(x_w[c][:], x_win[:].indirect(entries(offs_t, c * HALF, HALF)))
+        d_got = keep.tile([P, H], U32, name="d_got", tag="d_got", align_bytes=64)
+        nc.vector.tensor_copy(d_got[:], d_win[:].indirect(k1_t[:]))
+        d_w = keep.tile([P, H], U32, name="d_w", tag="d_w", align_bytes=64)
         nc.vector.tensor_copy(dealt_dst(d_w[:])[:, 0, :], dealt_src(d_got[:])[:, 0, :])
-        nc.vector.tensor_copy(x_w[0][:], x_win[:].indirect(entries(offs_t, 0, HALF)))
-        nc.vector.tensor_copy(dealt_dst(d_sc[:])[:, 0, :], dealt_src(d_sc_placed[:])[:, 0, :])
-        nc.vector.tensor_copy(x_w[1][:], x_win[:].indirect(entries(offs_t, HALF, HALF)))
 
         def first_product(t, c, acc):
             nc.tensor.matmul_mx(
@@ -123,12 +110,13 @@ def tile_picked_pqmixeodebl_none_po_kernel(
             )
 
         h = [keep.tile([P, S], F32, name=f"h{t}") for t in range(PACK)]
+        halves = [psum.tile([P, HALF], F32, name="acc", tag="acc") for c in range(2)]
         for c in range(2):
-            acc = psum.tile([P, HALF], F32, name="acc", tag="acc")
-            first_product(0, c, acc[:])
-            nc.vector.tensor_scalar(h[0][:, c * HALF : (c + 1) * HALF], acc[:], 0.0625, None, ALU.mult)
+            first_product(0, c, halves[c][:])
         nc.vector.tensor_copy(dealt_dst(d_w[:])[:, 1:, :], dealt_src(d_got[:])[:, 1:, :])
-        nc.vector.tensor_copy(dealt_dst(d_sc[:])[:, 1:, :], dealt_src(d_sc_placed[:])[:, 1:, :])
+        bias1 = gate_bias("bias1", sl_t, th_t, "d_got")
+        for c in range(2):
+            nc.vector.tensor_scalar(h[0][:, c * HALF : (c + 1) * HALF], halves[c][:], 0.0625, None, ALU.mult)
         for t in range(1, PACK):
             acc = psum.tile([P, S], F32, name="acc", tag="acc")
             for c in range(2):
@@ -138,61 +126,84 @@ def tile_picked_pqmixeodebl_none_po_kernel(
         two_t = load_list("two_t", two)
         n3_t = load_list("n3_t", n3)
         n4_t = load_list("n4_t", n4)
-        sl2_t = load_rows(nc.gpsimd, "sl2_t", sl2)
-        th2_t = load_rows(nc.gpsimd, "th2_t", th2)
-        bias2 = gate_bias("bias2", sl2_t, th2_t)
+        gn_t = load_rows(nc.sync, "gn_t", gn, "x_w0")
+        sl2_t = load_rows(nc.sync, "sl2_t", sl2, "d_sc")
+        th2_t = load_rows(nc.sync, "th2_t", th2, "x_w1")
 
-        w_raw = keep.tile([P, 2, N], U32, name="w_raw", tag="big")
-        for i, dram in enumerate((w2_words, w1_words)):
-            nc.sync.dma_start(w_raw[:, i, :].bitcast(I32), words_view(dram))
+        w1_raw = keep.tile([P, N], U32, name="w1_raw", tag="big", align_bytes=64)
+        nc.sync.dma_start(w1_raw[:].bitcast(I32), words_view(w1_words))
+        w2_raw = keep.tile([P, N], U32, name="w2_raw", tag="d_w", align_bytes=64)
+        nc.sync.dma_start(w2_raw[:].bitcast(I32), words_view(w2_words))
+        w_sc_raw = keep.tile([P, N], U8, name="w_sc_raw", tag="w_sc_raw", align_bytes=64)
+        nc.gpsimd.memset(w_sc_raw[:].bitcast(I32), 0)
+        for i, dram in enumerate((w1_scales, w2_scales)):
+            for q in range(4):
+                nc.sync.dma_start(
+                    w_sc_raw[:].bitcast(I32)[32 * q + 4 * i : 32 * q + 4 * i + 4, :],
+                    dram[0].bitcast(I32)[4 * q : 4 * q + 4, :],
+                )
 
-        z = [keep.tile([P, HALF, PACK], BF16, name=f"z{c}", align_bytes=64) for c in range(2)]
+        ra_tags = ("ra0", "ra1", "ra2", "w_sc_raw")
+        rb_tags = ("rb0", "rb1", "rb2", "big")
+        ra, rb, dt = {}, {}, {}
 
-        def stage_one(t, picked_tag, ra_tag, rb_tag):
-            scale, bias = sl_t[:, t : t + 1], bias1[:, t : t + 1]
-            sg2 = keep.tile([P, W], F32, name=f"sg2_{t}")
-            picked = keep.tile([P, 2, W], F32, name=f"picked{t}", tag=picked_tag)
-            pa, pb = picked[:, 0, :], picked[:, 1, :]
-            sg = keep.tile([P, W], F32, name=f"sg{t}")
-            ra = keep.tile([P, W], F32, name=f"ra{t}", tag=ra_tag)
-            rb = keep.tile([P, W], F32, name=f"rb{t}", tag=rb_tag)
-            dt = keep.tile([P, S], F32, name=f"dt{t}")
-            nc.scalar.activation(sg2[:], h[t][:].indirect(n2_t[:]), ACT.Sigmoid, bias=bias, scale=scale)
-            nc.scalar.activation(pa, h[t][:].indirect(n1_t[:]), ACT.Copy)
-            nc.vector.tensor_tensor(ra[:], pa, sg2[:], ALU.mult)
-            nc.scalar.activation(sg[:], h[t][:].indirect(n1_t[:]), ACT.Sigmoid, bias=bias, scale=scale)
-            nc.scalar.activation(pb, h[t][:].indirect(n2_t[:]), ACT.Copy)
-            nc.vector.tensor_tensor(rb[:], pb, sg[:], ALU.subtract)
-            nc.scalar.activation(dt[:].indirect(n1_t[:]), ra[:], ACT.Copy)
-            nc.scalar.activation(dt[:].indirect(n2_t[:]), rb[:], ACT.Copy)
-            return dt
-
-        def round_z(t, dt, c):
-            nc.vector.tensor_scalar(
-                z[c][:, :, t], dt[:, c * HALF : (c + 1) * HALF], gn_t[:, t : t + 1], None, ALU.mult
+        def gate(out, t, lst):
+            nc.scalar.activation(
+                out, h[t][:].indirect(lst[:]), ACT.Sigmoid, bias=bias1[:, t : t + 1], scale=sl_t[:, t : t + 1]
             )
 
-        dt = stage_one(0, "bias1_prod", "ra0", "rb0")
-        for c in range(2):
-            round_z(0, dt, c)
+        def fetch(t):
+            fetched = keep.tile([P, 3, W], F32, name=f"fetched{t}", tag=f"fetched{t}", align_bytes=64)
+            sg2, pa, pb = (fetched[:, i, :] for i in range(3))
+            sg = keep.tile([P, W], F32, name=f"sg{t}", tag=f"sg{t}", align_bytes=64)
+            ra[t] = keep.tile([P, W], F32, name=f"ra{t}", tag=ra_tags[t], align_bytes=64)
+            rb[t] = keep.tile([P, W], F32, name=f"rb{t}", tag=rb_tags[t], align_bytes=64)
+            gate(sg2, t, n2_t)
+            nc.scalar.activation(pa, h[t][:].indirect(n1_t[:]), ACT.Copy)
+            nc.vector.tensor_tensor(ra[t][:], pa, sg2, ALU.mult)
+            gate(sg[:], t, n1_t)
+            nc.scalar.activation(pb, h[t][:].indirect(n2_t[:]), ACT.Copy)
+            nc.vector.tensor_tensor(rb[t][:], pb, sg[:], ALU.subtract)
 
-        x2_w = [keep.tile([P, HALF], U32, name=f"x2_w{c}", tag=f"x_w{c}", align_bytes=64) for c in range(2)]
-        x2_sc = keep.tile([P, S], U8, name="x2_sc", tag="x_sc", align_bytes=64)
+        def put_first(t):
+            dt[t] = keep.tile([P, S], F32, name=f"dt{t}")
+            nc.scalar.activation(dt[t][:].indirect(n1_t[:]), ra[t][:], ACT.Copy)
+
+        def put_second(t):
+            nc.scalar.activation(dt[t][:].indirect(n2_t[:]), rb[t][:], ACT.Copy)
+
+        def round_z(t, c):
+            nc.vector.tensor_scalar(
+                z[:, c, :, t], dt[t][:, c * HALF : (c + 1) * HALF], gn_t[:, t : t + 1], None, ALU.mult
+            )
+
+        fetch(0)
+        fetch(1)
+        x2_sc = keep.tile([P, S], U8, name="x2_sc", tag="sg0", align_bytes=64)
+        x2_w = keep.tile([P, 2, HALF], U32, name="x2_w", tag="fetched0", align_bytes=64)
         for c in range(2):
-            nc.vector.tensor_copy(x2_w[c][:], x_win[:].indirect(entries(two_t, c * HALF, HALF)))
             nc.vector.tensor_copy(x2_sc[:, c * HALF : (c + 1) * HALF], x_sc_win[:].indirect(entries(two_t, c * HALF, HALF)))
-
-        dt = stage_one(1, "picked1", "ra1", "rb1")
         for c in range(2):
-            round_z(1, dt, c)
-
-        w2_w = keep.tile([P, N], U32, name="w2_w", align_bytes=64)
-        w1_w = keep.tile([P, N], U32, name="w1_w", align_bytes=64)
-        w_sc = keep.tile([P, N], U8, name="w_sc", align_bytes=64)
-        nc.vector.tensor_copy(dealt_dst(w2_w[:]), dealt_src(w_raw[:, 0, :]))
+            nc.vector.tensor_copy(x2_w[:, c, :], x_win[:].indirect(entries(two_t, c * HALF, HALF)))
+        fetch(2)
+        w_sc = keep.tile([P, N], U8, name="w_sc", tag="sg1", align_bytes=64)
+        w1_w = keep.tile([P, N], U32, name="w1_w", tag="fetched1", align_bytes=64)
         nc.vector.tensor_copy(dealt_dst(w_sc[:]), dealt_src(w_sc_raw[:]))
-        nc.vector.tensor_copy(dealt_dst(w1_w[:]), dealt_src(w_raw[:, 1, :]))
+        nc.vector.tensor_copy(dealt_dst(w1_w[:]), dealt_src(w1_raw[:]))
+        fetch(3)
+        bias2 = gate_bias("bias2", sl2_t, th2_t, "sg2")
 
+        z = keep.tile([P, 2, HALF, PACK], BF16, name="z", tag="x_win", align_bytes=64)
+        put_first(0)
+        for t in range(PACK - 1):
+            put_first(t + 1)
+            put_second(t)
+            for c in range(2):
+                round_z(t, c)
+        put_second(PACK - 1)
+
+        w2_w = keep.tile([P, N], U32, name="w2_w", tag="w_sc_raw", align_bytes=64)
+        nc.vector.tensor_copy(dealt_dst(w2_w[:]), dealt_src(w2_raw[:]))
         acc2 = {}
         for c in range(2):
             for t in range(PACK):
@@ -201,24 +212,19 @@ def tile_picked_pqmixeodebl_none_po_kernel(
                     out=acc2[c, t][:],
                     lhsT=w2_w[:, t * P : (t + 1) * P].bitcast(FP8X4),
                     lhsT_scale=w_sc[4:P, t * P : (t + 1) * P],
-                    rhs=x2_w[c][:].bitcast(FP8X4),
+                    rhs=x2_w[:, c, :].bitcast(FP8X4),
                     rhs_scale=x2_sc[:, c * HALF : (c + 1) * HALF],
                     start=True,
                     stop=False,
                 )
 
-        dt = stage_one(2, "picked2", "x_sc_win", "x_win")
-        for c in range(2):
-            round_z(2, dt, c)
-        dt = stage_one(3, "picked3", "w_sc_raw", "big")
-
         h2 = [keep.tile([P, S], F32, name=f"h2_{t}") for t in range(PACK)]
         z_w = [keep.tile([P, HALF], U32, name=f"z_w{c}", align_bytes=64) for c in range(2)]
         z_sc = [keep.tile([P, HALF], U8, name=f"z_sc{c}", align_bytes=64) for c in range(2)]
         for c in range(2):
-            round_z(3, dt, c)
+            round_z(3, c)
             nc.vector.quantize_mx(
-                out=z_w[c][:].bitcast(FP8X4), scales=z_sc[c][:], in_=z[c][:].rearrange("p w j -> p (w j)")
+                out=z_w[c][:].bitcast(FP8X4), scales=z_sc[c][:], in_=z[:, c, :, :].rearrange("p w j -> p (w j)")
             )
         for t in range(PACK):
             for c in range(2):
@@ -242,6 +248,7 @@ def tile_picked_pqmixeodebl_none_po_kernel(
         out_rows = out_0.rearrange("(p t) j -> p t j", t=PACK)
         o_w = keep.tile([P, S], U32, name="o_w", align_bytes=64)
         o_sc = keep.tile([P, S], U8, name="o_sc", align_bytes=64)
+        results = []
         for ci, (j0, cw) in enumerate(CHUNKS):
             cols = slice(j0, j0 + cw)
             res = keep.tile([P, PACK, cw], F32, name=f"res{ci}")
@@ -266,10 +273,17 @@ def tile_picked_pqmixeodebl_none_po_kernel(
                     nc.vector.tensor_tensor(prod[:, rows, :], sg3[:, rows, :], diff[:, rows, :], ALU.mult)
                     nc.vector.tensor_tensor(res[:, rows, :], pa2[:, rows, :], prod[:, rows, :], ALU.add)
             nc.sync.dma_start(out_rows[:, :, cols], res[:])
+            results.append(res)
+        for ci, (j0, cw) in enumerate(CHUNKS):
+            cols = slice(j0, j0 + cw)
+            res = results[ci]
             rounded = keep.tile([P, cw, PACK], BF16, name=f"rounded{ci}", align_bytes=64)
             dst = rounded[:].rearrange("p (c i) t -> p c t i", i=4)
             src = res[:].rearrange("p t (c i) -> p c t i", i=4)
-            nc.vector.tensor_copy(dst, src)
+            if ci + 1 < len(CHUNKS):
+                nc.scalar.copy(dst, src)
+            else:
+                nc.vector.tensor_copy(dst, src)
             nc.vector.quantize_mx(
                 out=o_w[:, cols].bitcast(FP8X4), scales=o_sc[:, cols], in_=rounded[:].rearrange("p w j -> p (w j)")
             )

@@ -248,46 +248,50 @@ def tile_picked_pqmixeodebl_none_po_kernel(
         out_rows = out_0.rearrange("(p t) j -> p t j", t=PACK)
         o_w = keep.tile([P, S], U32, name="o_w", align_bytes=64)
         o_sc = keep.tile([P, S], U8, name="o_sc", align_bytes=64)
-        results = []
-        for ci, (j0, cw) in enumerate(CHUNKS):
+        def mix(ci):
+            j0, cw = CHUNKS[ci]
             cols = slice(j0, j0 + cw)
             res = keep.tile([P, PACK, cw], F32, name=f"res{ci}")
             pa2 = keep.tile([P, PACK, cw], F32, name=f"pa2_{ci}")
             sg3 = keep.tile([P, PACK, cw], F32, name=f"sg3_{ci}")
             diff = keep.tile([P, PACK, cw], F32, name=f"diff_{ci}")
             prod = keep.tile([P, PACK, cw], F32, name=f"prod_{ci}")
-            group = 2
-            for t in range(PACK):
-                picked = h2[t][:].indirect(entries(n3_t, j0, cw))
-                if ci == 0 and t < 2:
-                    nc.vector.tensor_copy(pa2[:, t, :], picked)
-                else:
-                    nc.scalar.activation(pa2[:, t, :], picked, ACT.Copy)
-                nc.scalar.activation(
-                    sg3[:, t, :], h2[t][:].indirect(entries(n4_t, j0, cw)), ACT.Sigmoid,
-                    bias=bias2[:, t : t + 1], scale=sl2_t[:, t : t + 1],
-                )
-                nc.vector.tensor_tensor(diff[:, t, :], h2[t][:, cols], pa2[:, t, :], ALU.subtract)
-                if (t + 1) % group == 0:
-                    rows = slice(t + 1 - group, t + 1)
+            group = HALF // cw
+            groups = [slice(t, t + group) for t in range(0, PACK, group)]
+            for pair in range(0, len(groups), 2):
+                both = groups[pair : pair + 2]
+                for t in range(both[0].start, both[-1].stop):
+                    picked = h2[t][:].indirect(entries(n3_t, j0, cw))
+                    if ci == 0 and t == 0:
+                        nc.vector.tensor_copy(pa2[:, t, :], picked)
+                    else:
+                        nc.scalar.activation(pa2[:, t, :], picked, ACT.Copy)
+                    nc.scalar.activation(
+                        sg3[:, t, :], h2[t][:].indirect(entries(n4_t, j0, cw)), ACT.Sigmoid,
+                        bias=bias2[:, t : t + 1], scale=sl2_t[:, t : t + 1],
+                    )
+                    nc.vector.tensor_tensor(diff[:, t, :], h2[t][:, cols], pa2[:, t, :], ALU.subtract)
+                for rows in both:
                     nc.vector.tensor_tensor(prod[:, rows, :], sg3[:, rows, :], diff[:, rows, :], ALU.mult)
+                for rows in both:
                     nc.vector.tensor_tensor(res[:, rows, :], pa2[:, rows, :], prod[:, rows, :], ALU.add)
             nc.sync.dma_start(out_rows[:, :, cols], res[:])
-            results.append(res)
-        for ci, (j0, cw) in enumerate(CHUNKS):
+            return res
+
+        def hand_on(ci, res, copy):
+            j0, cw = CHUNKS[ci]
             cols = slice(j0, j0 + cw)
-            res = results[ci]
             rounded = keep.tile([P, cw, PACK], BF16, name=f"rounded{ci}", align_bytes=64)
-            dst = rounded[:].rearrange("p (c i) t -> p c t i", i=4)
-            src = res[:].rearrange("p t (c i) -> p c t i", i=4)
-            if ci + 1 < len(CHUNKS):
-                nc.scalar.copy(dst, src)
-            else:
-                nc.vector.tensor_copy(dst, src)
+            copy(rounded[:], res[:].rearrange("p t j -> p j t"))
             nc.vector.quantize_mx(
                 out=o_w[:, cols].bitcast(FP8X4), scales=o_sc[:, cols], in_=rounded[:].rearrange("p w j -> p (w j)")
             )
             nc.sync.dma_start(words_view(out_1)[:, cols], o_w[:, cols].bitcast(I32))
+
+        first = mix(0)
+        hand_on(1, mix(1), nc.vector.tensor_copy)
+        hand_on(2, mix(2), nc.vector.tensor_copy)
+        hand_on(0, first, nc.scalar.copy)
         for q in range(4):
             nc.scalar.dma_start(
                 out_2[0].bitcast(I32)[4 * q : 4 * q + 4, :], o_sc[:].bitcast(I32)[32 * q : 32 * q + 4, :]

@@ -240,7 +240,7 @@ def tile_picked_pqmixeodebl_none_po_kernel(
         for t in range(PACK):
             for c in range(2):
                 dst = h2[t][:, c * HALF : (c + 1) * HALF]
-                if c == 0 or t == 0:
+                if c == 0:
                     nc.scalar.copy(dst, acc2[c, t][:])
                 else:
                     nc.vector.tensor_copy(dst, acc2[c, t][:])
@@ -262,7 +262,7 @@ def tile_picked_pqmixeodebl_none_po_kernel(
                 both = groups[pair : pair + 2]
                 for t in range(both[0].start, both[-1].stop):
                     picked = h2[t][:].indirect(entries(n3_t, j0, cw))
-                    if ci == 0 and t == 0:
+                    if ci == 0 and t < 3:
                         nc.vector.tensor_copy(pa2[:, t, :], picked)
                     else:
                         nc.scalar.activation(pa2[:, t, :], picked, ACT.Copy)
@@ -278,20 +278,20 @@ def tile_picked_pqmixeodebl_none_po_kernel(
             nc.sync.dma_start(out_rows[:, :, cols], res[:])
             return res
 
-        def hand_on(ci, res, copy):
+        def hand_on(ci, res):
             j0, cw = CHUNKS[ci]
             cols = slice(j0, j0 + cw)
             rounded = keep.tile([P, cw, PACK], BF16, name=f"rounded{ci}", align_bytes=64)
-            copy(rounded[:], res[:].rearrange("p t j -> p j t"))
+            nc.vector.tensor_copy(
+                rounded[:].rearrange("p (c i) t -> p c t i", i=4), res[:].rearrange("p t (c i) -> p c t i", i=4)
+            )
             nc.vector.quantize_mx(
                 out=o_w[:, cols].bitcast(FP8X4), scales=o_sc[:, cols], in_=rounded[:].rearrange("p w j -> p (w j)")
             )
             nc.sync.dma_start(words_view(out_1)[:, cols], o_w[:, cols].bitcast(I32))
 
-        first = mix(0)
-        hand_on(1, mix(1), nc.vector.tensor_copy)
-        hand_on(2, mix(2), nc.vector.tensor_copy)
-        hand_on(0, first, nc.scalar.copy)
+        for ci in range(len(CHUNKS)):
+            hand_on(ci, mix(ci))
         for q in range(4):
             nc.scalar.dma_start(
                 out_2[0].bitcast(I32)[4 * q : 4 * q + 4, :], o_sc[:].bitcast(I32)[32 * q : 32 * q + 4, :]

from contextlib import ExitStack

import concourse.mybir as mybir

K, T, S, N, G, H, W = 512, 1024, 512, 512, 2048, 512, 256
FLOPS = 3 * 2 * 512 * 512 * 512

F32 = mybir.dt.float32
BF16 = mybir.dt.bfloat16
I32 = mybir.dt.int32
U32 = mybir.dt.uint32
U16 = mybir.dt.uint16
U8 = mybir.dt.uint8
FP8X4 = mybir.dt.float8_e4m3fn_x4
ALU = mybir.AluOpType
ACT = mybir.ActivationFunctionType

P = 128
PACK = 4
HALF = S // 2
CHUNKS = ((0, 256), (256, 128), (384, 128))


def tile_picked_pqmixeodebl_none_po_kernel(
    tc, x_words, x_scales, d_words, d_scales, sl, th, gn, w1_words, w1_scales, w2_words, w2_scales,
    sl2, th2, offs, k1, n1, n2, two, n3, n4, out_0, out_1, out_2,
):
    nc = tc.nc

    def entries(lst, start, count):
        return lst[:, start // 16 : (start + count) // 16]

    def words_view(dram):
        return dram[0].rearrange("p n t -> p (n t)").bitcast(I32)

    def dealt_src(tile):
        return tile.rearrange("p (m t) -> p t m", t=PACK)

    def dealt_dst(tile):
        return tile.rearrange("p (t m) -> p t m", t=PACK)

    with ExitStack() as ctx:
        keep = ctx.enter_context(tc.tile_pool(name="keep", bufs=1))
        psum = ctx.enter_context(tc.psum_pool(name="psum", bufs=8))

        def load_list(name, dram):
            tile = keep.tile(list(dram.shape), U16, name=name)
            nc.sync.dma_start(tile[:], dram)
            return tile

        def load_rows(queue, name, dram, tag):
            tile = keep.tile([P, PACK], F32, name=name, tag=tag, align_bytes=64)
            queue.dma_start(tile[:], dram.rearrange("(p t) o -> p (t o)", t=PACK))
            return tile

        k1_t = load_list("k1_t", k1)
        d_sc_win = keep.tile([P, G], U8, name="d_sc_win")
        nc.scalar.dma_start(
            d_sc_win[:].bitcast(I32), d_scales[0].bitcast(I32).unsqueeze(1).broadcast_to([16, 8, G // 4])
        )
        offs_t = load_list("offs_t", offs)
        x_sc_win = keep.tile([P, T], U8, name="x_sc_win")
        for q in range(4):
            nc.sync.dma_start(
                x_sc_win[:].bitcast(I32)[32 * q : 32 * q + 32, :],
                x_scales[0].bitcast(I32)[4 * q : 4 * q + 4, :].unsqueeze(0).broadcast_to([8, 4, T // 4]),
            )
        x_win = keep.tile([P, T], U32, name="x_win", tag="x_win", align_bytes=64)
        nc.scalar.dma_start(x_win[:].bitcast(I32), words_view(x_words))
        d_win = keep.tile([P, G], U32, name="d_win", tag="big", align_bytes=64)
        nc.scalar.dma_start(d_win[:].bitcast(I32), words_view(d_words))
        n2_t = load_list("n2_t", n2)
        n1_t = load_list("n1_t", n1)
        d_sc = keep.tile([P, H], U8, name="d_sc", tag="d_sc", align_bytes=64)
        nc.vector.memset(d_sc[:].bitcast(I32), 0)
        sl_t = load_rows(nc.gpsimd, "sl_t", sl, "sl_t")
        th_t = load_rows(nc.gpsimd, "th_t", th, "th_t")

        def gate_bias(name, slope, threshold, tag):
            bias = keep.tile([P, PACK], F32, name=name, tag=tag, align_bytes=64)
            nc.vector.scalar_tensor_tensor(bias[:], slope[:], -1.0, threshold[:], ALU.mult, ALU.mult)
            return bias

        d_sc_got = keep.tile([P, H], U8, name="d_sc_got")
        nc.vector.tensor_copy(d_sc_got[:], d_sc_win[:].indirect(k1_t[:]))
        d_sc_dealt = keep.tile([P, H], U8, name="d_sc_dealt", tag="w_sc_raw", align_bytes=64)
        nc.vector.tensor_copy(dealt_dst(d_sc_dealt[:]), dealt_src(d_sc_got[:]))
        for j in range(4):
            nc.scalar.dma_start(d_sc[:].bitcast(I32)[j:P:32, :], d_sc_dealt[:].bitcast(I32)[8 * j : P : 32, :])

        x_sc = keep.tile([P, S], U8, name="x_sc", align_bytes=64)
        nc.vector.tensor_copy(x_sc[:], x_sc_win[:].indirect(offs_t[:]))
        x_w = [keep.tile([P, HALF], U32, name=f"x_w{c}", tag=f"x_w{c}", align_bytes=64) for c in range(2)]
        for c in range(2):
            nc.vector.tensor_copy(x_w[c][:], x_win[:].indirect(entries(offs_t, c * HALF, HALF)))
        d_got = keep.tile([P, H], U32, name="d_got", tag="d_got", align_bytes=64)
        nc.vector.tensor_copy(d_got[:], d_win[:].indirect(k1_t[:]))
        d_w = keep.tile([P, H], U32, name="d_w", tag="d_w", align_bytes=64)
        nc.vector.tensor_copy(dealt_dst(d_w[:])[:, 0, :], dealt_src(d_got[:])[:, 0, :])

        def first_product(t, c, acc):
            nc.tensor.matmul_mx(
                out=acc,
                lhsT=d_w[:, t * P : (t + 1) * P].bitcast(FP8X4),
                lhsT_scale=d_sc[:, t * P : (t + 1) * P],
                rhs=x_w[c][:].bitcast(FP8X4),
                rhs_scale=x_sc[:, c * HALF : (c + 1) * HALF],
                start=True,
                stop=True,
            )

        h = [keep.tile([P, S], F32, name=f"h{t}") for t in range(PACK)]
        halves = [psum.tile([P, HALF], F32, name="acc", tag="acc") for c in range(2)]
        for c in range(2):
            first_product(0, c, halves[c][:])
        nc.vector.tensor_copy(dealt_dst(d_w[:])[:, 1:, :], dealt_src(d_got[:])[:, 1:, :])
        bias1 = gate_bias("bias1", sl_t, th_t, "d_got")
        for c in range(2):
            nc.vector.tensor_scalar(h[0][:, c * HALF : (c + 1) * HALF], halves[c][:], 0.0625, None, ALU.mult)
        for t in range(1, PACK):
            acc = psum.tile([P, S], F32, name="acc", tag="acc")
            for c in range(2):
                first_product(t, c, acc[:, c * HALF : (c + 1) * HALF])
            nc.vector.tensor_scalar(h[t][:], acc[:], 0.0625, None, ALU.mult)

        two_t = load_list("two_t", two)
        n3_t = load_list("n3_t", n3)
        n4_t = load_list("n4_t", n4)
        gn_t = load_rows(nc.sync, "gn_t", gn, "x_w0")
        sl2_t = load_rows(nc.sync, "sl2_t", sl2, "d_sc")
        th2_t = load_rows(nc.sync, "th2_t", th2, "x_w1")

        w1_raw = keep.tile([P, N], U32, name="w1_raw", tag="big", align_bytes=64)
        nc.sync.dma_start(w1_raw[:].bitcast(I32), words_view(w1_words))
        w2_raw = keep.tile([P, N], U32, name="w2_raw", tag="d_w", align_bytes=64)
        nc.sync.dma_start(w2_raw[:].bitcast(I32), words_view(w2_words))
        w_sc_raw = keep.tile([P, N], U8, name="w_sc_raw", tag="w_sc_raw", align_bytes=64)
        nc.gpsimd.memset(w_sc_raw[:].bitcast(I32), 0)
        for i, dram in enumerate((w1_scales, w2_scales)):
            for q in range(4):
                nc.sync.dma_start(
                    w_sc_raw[:].bitcast(I32)[32 * q + 4 * i : 32 * q + 4 * i + 4, :],
                    dram[0].bitcast(I32)[4 * q : 4 * q + 4, :],
                )

        ra_tags = ("ra0", "ra1", "ra2", "w_sc_raw")
        rb_tags = ("rb0", "rb1", "rb2", "big")
        ra, rb, dt = {}, {}, {}

        def gate(out, t, lst):
            nc.scalar.activation(
                out, h[t][:].indirect(lst[:]), ACT.Sigmoid, bias=bias1[:, t : t + 1], scale=sl_t[:, t : t + 1]
            )

        def fetch(t):
            fetched = keep.tile([P, 3, W], F32, name=f"fetched{t}", tag=f"fetched{t}", align_bytes=64)
            sg2, pa, pb = (fetched[:, i, :] for i in range(3))
            sg = keep.tile([P, W], F32, name=f"sg{t}", tag=f"sg{t}", align_bytes=64)
            ra[t] = keep.tile([P, W], F32, name=f"ra{t}", tag=ra_tags[t], align_bytes=64)
            rb[t] = keep.tile([P, W], F32, name=f"rb{t}", tag=rb_tags[t], align_bytes=64)
            gate(sg2, t, n2_t)
            nc.scalar.activation(pa, h[t][:].indirect(n1_t[:]), ACT.Copy)
            nc.vector.tensor_tensor(ra[t][:], pa, sg2, ALU.mult)
            gate(sg[:], t, n1_t)
            nc.scalar.activation(pb, h[t][:].indirect(n2_t[:]), ACT.Copy)
            nc.vector.tensor_tensor(rb[t][:], pb, sg[:], ALU.subtract)

        def put_first(t):
            dt[t] = keep.tile([P, S], F32, name=f"dt{t}")
            nc.scalar.activation(dt[t][:].indirect(n1_t[:]), ra[t][:], ACT.Copy)

        def put_second(t):
            nc.scalar.activation(dt[t][:].indirect(n2_t[:]), rb[t][:], ACT.Copy)

        def round_z(t, c):
            nc.vector.tensor_scalar(
                z[:, c, :, t], dt[t][:, c * HALF : (c + 1) * HALF], gn_t[:, t : t + 1], None, ALU.mult
            )

        fetch(0)
        fetch(1)
        x2_sc = keep.tile([P, S], U8, name="x2_sc", tag="sg0", align_bytes=64)
        x2_w = keep.tile([P, 2, HALF], U32, name="x2_w", tag="fetched0", align_bytes=64)
        for c in range(2):
            nc.vector.tensor_copy(x2_sc[:, c * HALF : (c + 1) * HALF], x_sc_win[:].indirect(entries(two_t, c * HALF, HALF)))
        for c in range(2):
            nc.vector.tensor_copy(x2_w[:, c, :], x_win[:].indirect(entries(two_t, c * HALF, HALF)))
        fetch(2)
        w_sc = keep.tile([P, N], U8, name="w_sc", tag="sg1", align_bytes=64)
        w1_w = keep.tile([P, N], U32, name="w1_w", tag="fetched1", align_bytes=64)
        nc.vector.tensor_copy(dealt_dst(w_sc[:]), dealt_src(w_sc_raw[:]))
        nc.vector.tensor_copy(dealt_dst(w1_w[:]), dealt_src(w1_raw[:]))
        fetch(3)
        bias2 = gate_bias("bias2", sl2_t, th2_t, "sg2")

        z = keep.tile([P, 2, HALF, PACK], BF16, name="z", tag="x_win", align_bytes=64)
        put_first(0)
        for t in range(PACK - 1):
            put_first(t + 1)
            put_second(t)
            for c in range(2):
                round_z(t, c)
        put_second(PACK - 1)

        w2_w = keep.tile([P, N], U32, name="w2_w", tag="w_sc_raw", align_bytes=64)
        nc.vector.tensor_copy(dealt_dst(w2_w[:]), dealt_src(w2_raw[:]))
        acc2 = {}
        for c in range(2):
            for t in range(PACK):
                acc2[c, t] = psum.tile([P, HALF], F32, name="acc", tag="acc")
                nc.tensor.matmul_mx(
                    out=acc2[c, t][:],
                    lhsT=w2_w[:, t * P : (t + 1) * P].bitcast(FP8X4),
                    lhsT_scale=w_sc[4:P, t * P : (t + 1) * P],
                    rhs=x2_w[:, c, :].bitcast(FP8X4),
                    rhs_scale=x2_sc[:, c * HALF : (c + 1) * HALF],
                    start=True,
                    stop=False,
                )

        h2 = [keep.tile([P, S], F32, name=f"h2_{t}") for t in range(PACK)]
        z_w = [keep.tile([P, HALF], U32, name=f"z_w{c}", align_bytes=64) for c in range(2)]
        z_sc = [keep.tile([P, HALF], U8, name=f"z_sc{c}", align_bytes=64) for c in range(2)]
        for c in range(2):
            round_z(3, c)
            nc.vector.quantize_mx(
                out=z_w[c][:].bitcast(FP8X4), scales=z_sc[c][:], in_=z[:, c, :, :].rearrange("p w j -> p (w j)")
            )
        for t in range(PACK):
            for c in range(2):
                nc.tensor.matmul_mx(
                    out=acc2[c, t][:],
                    lhsT=w1_w[:, t * P : (t + 1) * P].bitcast(FP8X4),
                    lhsT_scale=w_sc[:, t * P : (t + 1) * P],
                    rhs=z_w[c][:].bitcast(FP8X4),
                    rhs_scale=z_sc[c][:],
                    start=False,
                    stop=True,
                )
        for t in range(PACK):
            for c in range(2):
                dst = h2[t][:, c * HALF : (c + 1) * HALF]
                if c == 0:
                    nc.scalar.copy(dst, acc2[c, t][:])
                else:
                    nc.vector.tensor_copy(dst, acc2[c, t][:])

        out_rows = out_0.rearrange("(p t) j -> p t j", t=PACK)
        o_w = keep.tile([P, S], U32, name="o_w", align_bytes=64)
        o_sc = keep.tile([P, S], U8, name="o_sc", align_bytes=64)
        def mix(ci):
            j0, cw = CHUNKS[ci]
            cols = slice(j0, j0 + cw)
            res = keep.tile([P, PACK, cw], F32, name=f"res{ci}")
            pa2 = keep.tile([P, PACK, cw], F32, name=f"pa2_{ci}")
            sg3 = keep.tile([P, PACK, cw], F32, name=f"sg3_{ci}")
            diff = keep.tile([P, PACK, cw], F32, name=f"diff_{ci}")
            prod = keep.tile([P, PACK, cw], F32, name=f"prod_{ci}")
            group = HALF // cw
            groups = [slice(t, t + group) for t in range(0, PACK, group)]
            for pair in range(0, len(groups), 2):
                both = groups[pair : pair + 2]
                for t in range(both[0].start, both[-1].stop):
                    picked = h2[t][:].indirect(entries(n3_t, j0, cw))
                    if ci == 0 and t < 3:
                        nc.vector.tensor_copy(pa2[:, t, :], picked)
                    else:
                        nc.scalar.activation(pa2[:, t, :], picked, ACT.Copy)
                    nc.scalar.activation(
                        sg3[:, t, :], h2[t][:].indirect(entries(n4_t, j0, cw)), ACT.Sigmoid,
                        bias=bias2[:, t : t + 1], scale=sl2_t[:, t : t + 1],
                    )
                    nc.vector.tensor_tensor(diff[:, t, :], h2[t][:, cols], pa2[:, t, :], ALU.subtract)
                for rows in both:
                    nc.vector.tensor_tensor(prod[:, rows, :], sg3[:, rows, :], diff[:, rows, :], ALU.mult)
                for rows in both:
                    nc.vector.tensor_tensor(res[:, rows, :], pa2[:, rows, :], prod[:, rows, :], ALU.add)
            nc.sync.dma_start(out_rows[:, :, cols], res[:])
            return res

        def hand_on(ci, res):
            j0, cw = CHUNKS[ci]
            cols = slice(j0, j0 + cw)
            rounded = keep.tile([P, cw, PACK], BF16, name=f"rounded{ci}", align_bytes=64)
            nc.vector.tensor_copy(
                rounded[:].rearrange("p (c i) t -> p c t i", i=4), res[:].rearrange("p t (c i) -> p c t i", i=4)
            )
            nc.vector.quantize_mx(
                out=o_w[:, cols].bitcast(FP8X4), scales=o_sc[:, cols], in_=rounded[:].rearrange("p w j -> p (w j)")
            )
            nc.sync.dma_start(words_view(out_1)[:, cols], o_w[:, cols].bitcast(I32))

        for ci in range(len(CHUNKS)):
            hand_on(ci, mix(ci))
        for q in range(4):
            nc.scalar.dma_start(
                out_2[0].bitcast(I32)[4 * q : 4 * q + 4, :], o_sc[:].bitcast(I32)[32 * q : 32 * q + 4, :]
            )
